import numpy as np
import ml_dtypes


def mxq(x, axis, fmt="e4m3"):
    dtype, down = {"e4m3": (ml_dtypes.float8_e4m3fn, 7), "e5m2": (ml_dtypes.float8_e5m2, 14)}[fmt]
    v = np.moveaxis(np.asarray(x, np.float32).astype(ml_dtypes.bfloat16).astype(np.float64), axis, -1)
    blocks = v.reshape(v.shape[:-1] + (-1, 32))
    amax = np.abs(blocks).max(-1, keepdims=True)
    byte = np.maximum(np.where(amax > 0, np.frexp(amax)[1] - 1 + 127, 0) - down, 1)
    scale = np.exp2(byte - 127.0)
    codes = (blocks / scale).astype(np.float32).astype(dtype).astype(np.float64)
    return np.moveaxis((codes * scale).reshape(v.shape), -1, axis)


WIDE = False


def mx_kscale(k):
    if not WIDE:
        return np.ones(k)
    levels = np.array([10, -10, 5, -5, 0])
    if k % 512:
        return np.exp2(np.random.permutation(np.resize(levels, k // 32))).repeat(32)
    a = np.empty((k // 512, 16))
    for p in range(k // 512):
        a[p, :8] = np.random.permutation(np.resize(levels, 8))
        for g in range(8):
            far = levels[np.abs(levels - a[p, g]) >= 10]
            a[p, g + 8] = far[np.random.randint(len(far))]
    return np.exp2(a.ravel()).repeat(32)


BF16 = ml_dtypes.bfloat16


def bf(x):
    return np.asarray(x, np.float32).astype(BF16)


def f64(x):
    return np.asarray(x).astype(np.float64)


E2M1 = np.array([0.0, 0.5, 1.0, 1.5, 2.0, 3.0, 4.0, 6.0, -0.0, -0.5, -1.0, -1.5, -2.0, -3.0, -4.0, -6.0])


def pack_weight(w, fmt):
    k, n = w.shape
    w = f64(bf(w)).reshape(k // 32, 32, n)
    amax = np.abs(w).max(1)
    if fmt == "e4m3":
        byte = np.frexp(amax)[1] - 1 + 127 - 7
    else:
        mant, ex = np.frexp(amax / 6.0)
        byte = np.where(mant > 0.5, ex, ex - 1) + 127
    byte = np.clip(np.where(amax > 0, byte, 1), 1, 254)
    scaled = (w * np.exp2(127.0 - byte)[:, None, :]).reshape(k, n).astype(np.float32)
    by_word = np.ascontiguousarray(scaled.reshape(k // 512, 128, 4, n).transpose(0, 1, 3, 2))
    if fmt == "e4m3":
        words = by_word.astype(ml_dtypes.float8_e4m3fn).view(np.uint8)
    else:
        c = by_word.astype(ml_dtypes.float4_e2m1fn).view(np.uint8) & 0xF
        words = c[..., 0::2] | (c[..., 1::2] << 4)
    return np.ascontiguousarray(words), np.ascontiguousarray(byte.astype(np.uint8).reshape(k // 512, 16, n))


def unpack_weight(words, scales, fmt):
    g, p, n, _ = words.shape
    if fmt == "e4m3":
        vals = np.ascontiguousarray(words).view(ml_dtypes.float8_e4m3fn).astype(np.float64)
    else:
        nib = np.empty((g, p, n, 4), np.uint8)
        nib[..., 0::2] = words & 0xF
        nib[..., 1::2] = words >> 4
        vals = E2M1[nib]
    vals = vals * np.repeat(np.exp2(scales.astype(np.float64) - 127.0), 8, axis=1)[..., None]
    return vals.transpose(0, 1, 3, 2).reshape(g * 512, n)
def pack4(w):
    words, scales = pack_weight(w, "e2m1")
    return words.reshape(words.shape[0], 128, -1), scales


def unpack4(words, scales):
    return unpack_weight(words.reshape(words.shape[0], 128, -1, 2), scales, "e2m1")


N, F = 2048, 512


def setup_inputs():
    s = mx_kscale(N)
    d = 1 + 0.1 * np.random.standard_normal(N)
    w_words, w_scales = pack4(np.random.standard_normal((N, N)) / np.sqrt(N) / s[:, None])
    return {"x": bf(np.random.standard_normal((N, F)) * s[:, None]),
            "w_words": w_words,
            "w_scales": w_scales,
            "twice_inv_deg": bf(2.0 / d * s),
            "deg": bf(d / s)}


def reference(x, w_words, w_scales, twice_inv_deg, deg):
    x = f64(x)
    w = unpack4(w_words, w_scales)
    h = w.T @ mxq(x, 0, "e4m3")
    h = h * f64(twice_inv_deg)[:, None]
    y = w.T @ mxq(h, 0, "e4m3")
    return y - f64(deg)[:, None] * x

@@ -1,0 +1,224 @@
+from contextlib import ExitStack
+
+import concourse.mybir as mybir
+from concourse.masks import make_identity
+
+N, F = 2048, 512
+FLOPS = 2 * 2 * N * N * F
+
+F32 = mybir.dt.float32
+BF16 = mybir.dt.bfloat16
+I32 = mybir.dt.int32
+U32 = mybir.dt.uint32
+U8 = mybir.dt.uint8
+FP8X4 = mybir.dt.float8_e4m3fn_x4
+FP4X4 = mybir.dt.float4_e2m1fn_x4
+MULT = mybir.AluOpType.mult
+ADD = mybir.AluOpType.add
+COPY = mybir.ActivationFunctionType.Copy
+
+P = 128
+PACK = 4
+K_PASS = P * PACK
+PASSES = N // K_PASS
+TILES = N // P
+BANKS = 8
+HALF = BANKS * P
+
+
+def interleave(copy, grouped, raw, lo, hi):
+    copy(
+        out=grouped[:, lo:hi, :].rearrange("p (c i) t -> p c t i", i=4),
+        in_=raw.rearrange("p t (c i) -> p c t i", i=4),
+    )
+
+
+def tile_chebyshev_graph_filter_s13_kernel(tc, x, w_words, w_scales, twice_inv_deg, deg, out):
+    nc = tc.nc
+    with ExitStack() as ctx:
+        sb = ctx.enter_context(tc.tile_pool(name="sb", bufs=1))
+        ps = ctx.enter_context(tc.psum_pool(name="ps", bufs=1))
+        ctx.enter_context(tc.manual_schedule())
+
+        banks = [ps.tile([P, F], F32, name="bank%d" % b) for b in range(BANKS)]
+        parked = out[0 : N // 2, :].bitcast(BF16).rearrange("r (two w) -> (r two) w", two=2)
+
+        first_scales = sb.tile([P, HALF], U8, align_bytes=64)
+        early_scales = sb.tile([P, PASSES - 1, HALF], U8, align_bytes=64)
+        late_scales = sb.tile([P, PASSES, HALF], U8, align_bytes=64)
+        early_w = [sb.tile([P, 2 * HALF], U8, name="early_w%d" % g, align_bytes=64) for g in range(PASSES)]
+        late_w = [sb.tile([P, PASSES, HALF], U8, name="late_w%d" % h, align_bytes=64) for h in range(2)]
+        x_first = [sb.tile([P, PACK, F // 2], BF16, name="x_first%d" % h) for h in range(2)]
+        x_raw = [sb.tile([P, PACK, F], BF16, name="x_raw%d" % g) for g in range(1, PASSES)]
+        x_rows = [sb.tile([P, PACK, F], BF16, name="x_rows%d" % g) for g in range(PASSES)]
+        x_grouped = [sb.tile([P, F, PACK], BF16, name="x_grouped%d" % g, align_bytes=64) for g in range(PASSES)]
+        x_codes = [sb.tile([P, F], U32, name="x_codes%d" % g, align_bytes=64) for g in range(PASSES)]
+        x_scales = [sb.tile([P, F], U8, name="x_scales%d" % g, align_bytes=64) for g in range(PASSES)]
+        h_rows = [sb.tile([P, F], BF16, name="h_rows%d" % t) for t in range(TILES)]
+        h_raw = [sb.tile([P, PACK * F], BF16, name="h_raw%d" % g) for g in range(PASSES)]
+        h_grouped = [sb.tile([P, F, PACK], BF16, name="h_grouped%d" % g, align_bytes=64) for g in range(PASSES)]
+        h_codes = [sb.tile([P, F], U32, name="h_codes%d" % g, align_bytes=64) for g in range(PASSES)]
+        h_scales = [sb.tile([P, F], U8, name="h_scales%d" % g, align_bytes=64) for g in range(PASSES)]
+        y_rows = [sb.tile([P, F], F32, name="y_rows%d" % t) for t in range(TILES)]
+        factor_rows = sb.tile([P, P], BF16)
+        identity = sb.tile([P, P], BF16)
+        gain = sb.tile([P, TILES], F32)
+        minus_deg = sb.tile([P, TILES], F32)
+
+        def w_operand(g, t):
+            if t < BANKS:
+                codes = early_w[g][:, 2 * P * t : 2 * P * (t + 1)]
+                cols = slice(P * t, P * (t + 1))
+                scales = first_scales[:, cols] if g == 0 else early_scales[:, g - 1, cols]
+            else:
+                u = t - BANKS
+                codes = late_w[u // 4][:, g, 2 * P * (u % 4) : 2 * P * (u % 4 + 1)]
+                scales = late_scales[:, g, P * u : P * (u + 1)]
+            return codes.bitcast(FP4X4), scales
+
+        def mx_pass(t, g, codes, scales):
+            w_codes, w_plane = w_operand(g, t)
+            nc.tensor.matmul_mx(
+                out=banks[t % BANKS][:],
+                lhsT=w_codes,
+                lhsT_scale=w_plane,
+                rhs=codes[g][:].bitcast(FP8X4),
+                rhs_scale=scales[g][:],
+                start=(g == 0),
+                stop=(g == PASSES - 1),
+            )
+
+        def quantise(grouped, codes, scales, lo, hi):
+            nc.vector.quantize_mx(
+                out=codes[:, lo:hi].bitcast(FP8X4),
+                scales=scales[:, lo:hi],
+                in_=grouped[:, lo:hi, :].rearrange("p f t -> p (f t)"),
+            )
+
+        def load_scales(plane, passes, cols):
+            rows = w_scales.rearrange("g (q r) n -> r q g n", r=4)
+            for r in range(4):
+                nc.sync.dma_start(out=plane[r:P:32].bitcast(I32), in_=rows[r][:, passes, cols].bitcast(I32))
+
+        nc.vector.memset(first_scales[:].bitcast(I32), 0)
+        nc.vector.memset(early_scales[:].rearrange("p g n -> p (g n)").bitcast(I32), 0)
+        nc.vector.memset(late_scales[:].rearrange("p g n -> p (g n)").bitcast(I32), 0)
+        nc.gpsimd.memset(factor_rows[32:64, :], 0.0)
+        nc.gpsimd.memset(factor_rows[64:P, :], 0.0)
+        make_identity(nc, identity[:])
+        nc.scalar.dma_start(out=factor_rows[0:TILES, :], in_=twice_inv_deg.rearrange("(t p) -> t p", p=P))
+        nc.scalar.dma_start(out=factor_rows[TILES : 2 * TILES, :], in_=deg.rearrange("(t p) -> t p", p=P))
+
+        x_by_word = x.rearrange("(g p t) f -> g p t f", p=P, t=PACK)
+        for h in range(2):
+            nc.sync.dma_start(out=x_first[h][:], in_=x_by_word[0][:, :, h * (F // 2) : (h + 1) * (F // 2)])
+        nc.sync.dma_start(out=early_w[0][:].bitcast(I32), in_=w_words[0][:, 0 : 2 * HALF].bitcast(I32))
+        load_scales(first_scales, 0, slice(0, HALF))
+        for g in range(1, PASSES):
+            nc.sync.dma_start(out=x_raw[g - 1][:], in_=x_by_word[g])
+            nc.sync.dma_start(out=early_w[g][:].bitcast(I32), in_=w_words[g][:, 0 : 2 * HALF].bitcast(I32))
+            if g == 1:
+                load_scales(early_scales, slice(1, PASSES), slice(0, HALF))
+        load_scales(late_scales, slice(0, PASSES), slice(HALF, N))
+        w_by_partition = w_words.rearrange("g p b -> p g b")
+        for h in range(2):
+            nc.sync.dma_start(
+                out=late_w[h][:].bitcast(I32),
+                in_=w_by_partition[:, :, (2 + h) * HALF : (3 + h) * HALF].bitcast(I32),
+            )
+        x_by_tile = x.rearrange("(g t p) f -> g p t f", p=P, t=PACK)
+        for g in range(PASSES):
+            nc.sync.dma_start(out=x_rows[g][:], in_=x_by_tile[g])
+
+        turned = banks[BANKS - 1][:].bitcast(BF16)[:, 0:P]
+        nc.tensor.transpose(turned, factor_rows[:], identity[:])
+
+        split = 176
+        for h in range(2):
+            lo = h * (F // 2)
+            interleave(nc.vector.tensor_copy, x_grouped[0], x_first[h][:, :, 0:split], lo, lo + split)
+            interleave(nc.scalar.copy, x_grouped[0], x_first[h][:, :, split : F // 2], lo + split, lo + F // 2)
+        for h in range(2):
+            quantise(x_grouped[0], x_codes[0], x_scales[0], h * (F // 2), (h + 1) * (F // 2))
+        nc.scalar.activation(out=gain[:], in_=turned[:, 0:TILES], func=COPY)
+        nc.scalar.activation(out=minus_deg[:], in_=turned[:, TILES : 2 * TILES], func=COPY, scale=-1.0)
+        for g in range(1, PASSES):
+            interleave(nc.vector.tensor_copy, x_grouped[g], x_raw[g - 1][:, :, 0 : F // 2], 0, F // 2)
+            interleave(nc.scalar.copy, x_grouped[g], x_raw[g - 1][:, :, F // 2 : F], F // 2, F)
+            quantise(x_grouped[g], x_codes[g], x_scales[g], 0, F)
+
+        def scale_and_park(t, on_vector):
+            if on_vector:
+                nc.vector.tensor_scalar(
+                    out=h_rows[t][:], in0=banks[t % BANKS][:], scalar1=gain[:, t : t + 1], scalar2=None, op0=MULT
+                )
+            else:
+                nc.scalar.activation(out=h_rows[t][:], in_=banks[t % BANKS][:], func=COPY, scale=gain[:, t : t + 1])
+            if t < TILES - 2:
+                nc.sync.dma_start(out=parked[P * t : P * (t + 1), :], in_=h_rows[t][:])
+            else:
+                q = t % PACK
+                for j in range(PACK):
+                    nc.sync.dma_start(
+                        out=h_raw[t // PACK][32 * q : 32 * (q + 1), F * j : F * (j + 1)], in_=h_rows[t][j:P:PACK, :]
+                    )
+
+        def fetch(g, lo, hi):
+            rows = parked[K_PASS * g + PACK * lo : K_PASS * g + PACK * hi, :]
+            nc.sync.dma_start(
+                out=h_raw[g][lo:hi, :], in_=rows.rearrange("(p t) w -> p (t w)", t=PACK)
+            )
+
+        def quantise_h(g, split):
+            raw = h_raw[g][:].rearrange("p (t f) -> p t f", t=PACK)
+            interleave(nc.vector.tensor_copy, h_grouped[g], raw[:, :, 0:split], 0, split)
+            if split < F:
+                interleave(nc.scalar.copy, h_grouped[g], raw[:, :, split:F], split, F)
+            quantise(h_grouped[g], h_codes[g], h_scales[g], 0, F)
+
+        for g in range(PASSES):
+            for t in range(BANKS):
+                mx_pass(t, g, x_codes, x_scales)
+        for t in range(BANKS):
+            scale_and_park(t, t % 2 == 1)
+        for t in range(BANKS, TILES):
+            for g in range(PASSES):
+                mx_pass(t, g, x_codes, x_scales)
+            if t == 8:
+                fetch(0, 0, P)
+                quantise_h(0, F)
+            if t == 9:
+                fetch(1, 0, P)
+                quantise_h(1, F)
+            if t == 14:
+                fetch(2, 0, P)
+                quantise_h(2, F)
+            if t == 15:
+                fetch(3, 0, 64)
+            scale_and_park(t, False)
+        quantise_h(3, 344)
+
+        def finish(t, lo, hi):
+            nc.vector.scalar_tensor_tensor(
+                out=y_rows[t][:, lo:hi],
+                in0=x_rows[t // PACK][:, t % PACK, lo:hi],
+                scalar=minus_deg[:, t : t + 1],
+                in1=banks[t % BANKS][:, lo:hi],
+                op0=MULT,
+                op1=ADD,
+            )
+            nc.sync.dma_start(out=out[P * t : P * (t + 1), lo:hi], in_=y_rows[t][:, lo:hi])
+
+        for g in range(PASSES):
+            for t in range(BANKS):
+                mx_pass(t, g, h_codes, h_scales)
+        for t in range(BANKS):
+            finish(t, 0, F)
+        for t in range(BANKS, TILES):
+            for g in range(PASSES):
+                mx_pass(t, g, h_codes, h_scales)
+            if t < TILES - 1:
+                finish(t, 0, F)
+            else:
+                finish(t, 0, F // 2)
+                finish(t, F // 2, F)

@@ -24,6 +24,7 @@ PASSES = N // K_PASS
 TILES = N // P
 BANKS = 8
 HALF = BANKS * P
+SHARE = 304
 
 
 def interleave(copy, grouped, raw, lo, hi):
@@ -48,8 +49,7 @@ def tile_chebyshev_graph_filter_s13_kernel(tc, x, w_words, w_scales, twice_inv_d
         late_scales = sb.tile([P, PASSES, HALF], U8, align_bytes=64)
         early_w = [sb.tile([P, 2 * HALF], U8, name="early_w%d" % g, align_bytes=64) for g in range(PASSES)]
         late_w = [sb.tile([P, PASSES, HALF], U8, name="late_w%d" % h, align_bytes=64) for h in range(2)]
-        x_first = [sb.tile([P, PACK, F // 2], BF16, name="x_first%d" % h) for h in range(2)]
-        x_raw = [sb.tile([P, PACK, F], BF16, name="x_raw%d" % g) for g in range(1, PASSES)]
+        x_raw = [sb.tile([P, PACK, F], BF16, name="x_raw%d" % g) for g in range(PASSES)]
         x_rows = [sb.tile([P, PACK, F], BF16, name="x_rows%d" % g) for g in range(PASSES)]
         x_grouped = [sb.tile([P, F, PACK], BF16, name="x_grouped%d" % g, align_bytes=64) for g in range(PASSES)]
         x_codes = [sb.tile([P, F], U32, name="x_codes%d" % g, align_bytes=64) for g in range(PASSES)]
@@ -110,12 +110,11 @@ def tile_chebyshev_graph_filter_s13_kernel(tc, x, w_words, w_scales, twice_inv_d
         nc.scalar.dma_start(out=factor_rows[TILES : 2 * TILES, :], in_=deg.rearrange("(t p) -> t p", p=P))
 
         x_by_word = x.rearrange("(g p t) f -> g p t f", p=P, t=PACK)
-        for h in range(2):
-            nc.sync.dma_start(out=x_first[h][:], in_=x_by_word[0][:, :, h * (F // 2) : (h + 1) * (F // 2)])
+        nc.sync.dma_start(out=x_raw[0][:], in_=x_by_word[0])
         nc.sync.dma_start(out=early_w[0][:].bitcast(I32), in_=w_words[0][:, 0 : 2 * HALF].bitcast(I32))
         load_scales(first_scales, 0, slice(0, HALF))
         for g in range(1, PASSES):
-            nc.sync.dma_start(out=x_raw[g - 1][:], in_=x_by_word[g])
+            nc.sync.dma_start(out=x_raw[g][:], in_=x_by_word[g])
             nc.sync.dma_start(out=early_w[g][:].bitcast(I32), in_=w_words[g][:, 0 : 2 * HALF].bitcast(I32))
             if g == 1:
                 load_scales(early_scales, slice(1, PASSES), slice(0, HALF))
@@ -126,26 +125,24 @@ def tile_chebyshev_graph_filter_s13_kernel(tc, x, w_words, w_scales, twice_inv_d
                 out=late_w[h][:].bitcast(I32),
                 in_=w_by_partition[:, :, (2 + h) * HALF : (3 + h) * HALF].bitcast(I32),
             )
-        x_by_tile = x.rearrange("(g t p) f -> g p t f", p=P, t=PACK)
-        for g in range(PASSES):
-            nc.sync.dma_start(out=x_rows[g][:], in_=x_by_tile[g])
 
         turned = banks[BANKS - 1][:].bitcast(BF16)[:, 0:P]
         nc.tensor.transpose(turned, factor_rows[:], identity[:])
 
-        split = 176
-        for h in range(2):
-            lo = h * (F // 2)
-            interleave(nc.vector.tensor_copy, x_grouped[0], x_first[h][:, :, 0:split], lo, lo + split)
-            interleave(nc.scalar.copy, x_grouped[0], x_first[h][:, :, split : F // 2], lo + split, lo + F // 2)
-        for h in range(2):
-            quantise(x_grouped[0], x_codes[0], x_scales[0], h * (F // 2), (h + 1) * (F // 2))
-        nc.scalar.activation(out=gain[:], in_=turned[:, 0:TILES], func=COPY)
-        nc.scalar.activation(out=minus_deg[:], in_=turned[:, TILES : 2 * TILES], func=COPY, scale=-1.0)
-        for g in range(1, PASSES):
-            interleave(nc.vector.tensor_copy, x_grouped[g], x_raw[g - 1][:, :, 0 : F // 2], 0, F // 2)
-            interleave(nc.scalar.copy, x_grouped[g], x_raw[g - 1][:, :, F // 2 : F], F // 2, F)
-            quantise(x_grouped[g], x_codes[g], x_scales[g], 0, F)
+        def pack_operand(raw, grouped, codes, scales, split):
+            half = F // 2
+            interleave(nc.vector.tensor_copy, grouped, raw[:, :, 0:half], 0, half)
+            interleave(nc.vector.tensor_copy, grouped, raw[:, :, half:split], half, split)
+            if split < F:
+                interleave(nc.scalar.copy, grouped, raw[:, :, split:F], split, F)
+            quantise(grouped, codes, scales, 0, half)
+            quantise(grouped, codes, scales, half, F)
+
+        for g in range(PASSES):
+            pack_operand(x_raw[g][:], x_grouped[g], x_codes[g], x_scales[g], SHARE)
+            if g == 0:
+                nc.scalar.activation(out=gain[:], in_=turned[:, 0:TILES], func=COPY)
+                nc.scalar.activation(out=minus_deg[:], in_=turned[:, TILES : 2 * TILES], func=COPY, scale=-1.0)
 
         def scale_and_park(t, on_vector):
             if on_vector:
@@ -171,10 +168,7 @@ def tile_chebyshev_graph_filter_s13_kernel(tc, x, w_words, w_scales, twice_inv_d
 
         def quantise_h(g, split):
             raw = h_raw[g][:].rearrange("p (t f) -> p t f", t=PACK)
-            interleave(nc.vector.tensor_copy, h_grouped[g], raw[:, :, 0:split], 0, split)
-            if split < F:
-                interleave(nc.scalar.copy, h_grouped[g], raw[:, :, split:F], split, F)
-            quantise(h_grouped[g], h_codes[g], h_scales[g], 0, F)
+            pack_operand(raw, h_grouped[g], h_codes[g], h_scales[g], split)
 
         for g in range(PASSES):
             for t in range(BANKS):
@@ -196,7 +190,10 @@ def tile_chebyshev_graph_filter_s13_kernel(tc, x, w_words, w_scales, twice_inv_d
             if t == 15:
                 fetch(3, 0, 64)
             scale_and_park(t, False)
-        quantise_h(3, 344)
+        x_by_tile = x.rearrange("(g t p) f -> g p t f", p=P, t=PACK)
+        for g in range(PASSES):
+            nc.sync.dma_start(out=x_rows[g][:], in_=x_by_tile[g])
+        quantise_h(3, SHARE)
 
         def finish(t, lo, hi):
             nc.vector.scalar_tensor_tensor(

@@ -25,6 +25,7 @@ TILES = N // P
 BANKS = 8
 HALF = BANKS * P
 SHARE = 304
+WARM_UP = 14
 
 
 def interleave(copy, grouped, raw, lo, hi):
@@ -44,8 +45,7 @@ def tile_chebyshev_graph_filter_s13_kernel(tc, x, w_words, w_scales, twice_inv_d
         banks = [ps.tile([P, F], F32, name="bank%d" % b) for b in range(BANKS)]
         parked = out[0 : N // 2, :].bitcast(BF16).rearrange("r (two w) -> (r two) w", two=2)
 
-        first_scales = sb.tile([P, HALF], U8, align_bytes=64)
-        early_scales = sb.tile([P, PASSES - 1, HALF], U8, align_bytes=64)
+        early_scales = [sb.tile([P, 2, HALF], U8, name="early_scales%d" % h, align_bytes=64) for h in range(2)]
         late_scales = sb.tile([P, PASSES, HALF], U8, align_bytes=64)
         early_w = [sb.tile([P, 2 * HALF], U8, name="early_w%d" % g, align_bytes=64) for g in range(PASSES)]
         late_w = [sb.tile([P, PASSES, HALF], U8, name="late_w%d" % h, align_bytes=64) for h in range(2)]
@@ -62,6 +62,9 @@ def tile_chebyshev_graph_filter_s13_kernel(tc, x, w_words, w_scales, twice_inv_d
         y_rows = [sb.tile([P, F], F32, name="y_rows%d" % t) for t in range(TILES)]
         factor_rows = sb.tile([P, P], BF16)
         identity = sb.tile([P, P], BF16)
+        zeros = sb.tile([P, P, PACK], BF16, align_bytes=64)
+        zero_codes = sb.tile([P, P], U32, align_bytes=64)
+        zero_scales = sb.tile([P, P], U8, align_bytes=64)
         gain = sb.tile([P, TILES], F32)
         minus_deg = sb.tile([P, TILES], F32)
 
@@ -69,7 +72,7 @@ def tile_chebyshev_graph_filter_s13_kernel(tc, x, w_words, w_scales, twice_inv_d
             if t < BANKS:
                 codes = early_w[g][:, 2 * P * t : 2 * P * (t + 1)]
                 cols = slice(P * t, P * (t + 1))
-                scales = first_scales[:, cols] if g == 0 else early_scales[:, g - 1, cols]
+                scales = early_scales[g // 2][:, g % 2, cols]
             else:
                 u = t - BANKS
                 codes = late_w[u // 4][:, g, 2 * P * (u % 4) : 2 * P * (u % 4 + 1)]
@@ -100,9 +103,11 @@ def tile_chebyshev_graph_filter_s13_kernel(tc, x, w_words, w_scales, twice_inv_d
             for r in range(4):
                 nc.sync.dma_start(out=plane[r:P:32].bitcast(I32), in_=rows[r][:, passes, cols].bitcast(I32))
 
-        nc.vector.memset(first_scales[:].bitcast(I32), 0)
-        nc.vector.memset(early_scales[:].rearrange("p g n -> p (g n)").bitcast(I32), 0)
-        nc.vector.memset(late_scales[:].rearrange("p g n -> p (g n)").bitcast(I32), 0)
+        nc.vector.memset(zeros[:], 0.0)
+        nc.vector.memset(early_scales[0][:].rearrange("p g n -> p (g n)").bitcast(I32), 0)
+        quantise(zeros, zero_codes, zero_scales, 0, P)
+        for plane in [early_scales[1], late_scales]:
+            nc.vector.memset(plane[:].rearrange("p g n -> p (g n)").bitcast(I32), 0)
         nc.gpsimd.memset(factor_rows[32:64, :], 0.0)
         nc.gpsimd.memset(factor_rows[64:P, :], 0.0)
         make_identity(nc, identity[:])
@@ -110,14 +115,13 @@ def tile_chebyshev_graph_filter_s13_kernel(tc, x, w_words, w_scales, twice_inv_d
         nc.scalar.dma_start(out=factor_rows[TILES : 2 * TILES, :], in_=deg.rearrange("(t p) -> t p", p=P))
 
         x_by_word = x.rearrange("(g p t) f -> g p t f", p=P, t=PACK)
-        nc.sync.dma_start(out=x_raw[0][:], in_=x_by_word[0])
-        nc.sync.dma_start(out=early_w[0][:].bitcast(I32), in_=w_words[0][:, 0 : 2 * HALF].bitcast(I32))
-        load_scales(first_scales, 0, slice(0, HALF))
-        for g in range(1, PASSES):
+        nc.sync.dma_start(out=early_w[0][:, 0 : 2 * P].bitcast(I32), in_=w_words[0][:, 0 : 2 * P].bitcast(I32))
+        for g in range(PASSES):
             nc.sync.dma_start(out=x_raw[g][:], in_=x_by_word[g])
-            nc.sync.dma_start(out=early_w[g][:].bitcast(I32), in_=w_words[g][:, 0 : 2 * HALF].bitcast(I32))
-            if g == 1:
-                load_scales(early_scales, slice(1, PASSES), slice(0, HALF))
+            rest = slice(2 * P if g == 0 else 0, 2 * HALF)
+            nc.sync.dma_start(out=early_w[g][:, rest].bitcast(I32), in_=w_words[g][:, rest].bitcast(I32))
+            if g % 2 == 0:
+                load_scales(early_scales[g // 2], slice(g, g + 2), slice(0, HALF))
         load_scales(late_scales, slice(0, PASSES), slice(HALF, N))
         w_by_partition = w_words.rearrange("g p b -> p g b")
         for h in range(2):
@@ -126,6 +130,16 @@ def tile_chebyshev_graph_filter_s13_kernel(tc, x, w_words, w_scales, twice_inv_d
                 in_=w_by_partition[:, :, (2 + h) * HALF : (3 + h) * HALF].bitcast(I32),
             )
 
+        for r in range(WARM_UP):
+            nc.tensor.matmul_mx(
+                out=banks[0][:, 0:P],
+                lhsT=early_w[0][:, 0 : 2 * P].bitcast(FP4X4),
+                lhsT_scale=zero_scales[:],
+                rhs=zero_codes[:].bitcast(FP8X4),
+                rhs_scale=zero_scales[:],
+                start=True,
+                stop=True,
+            )
         turned = banks[BANKS - 1][:].bitcast(BF16)[:, 0:P]
         nc.tensor.transpose(turned, factor_rows[:], identity[:])
 

@@ -26,6 +26,8 @@ BANKS = 8
 HALF = BANKS * P
 SHARE = 304
 WARM_UP = 14
+DIRECT = (11,)
+SORTED = TILES - PACK
 
 
 def interleave(copy, grouped, raw, lo, hi):
@@ -45,7 +47,7 @@ def tile_chebyshev_graph_filter_s13_kernel(tc, x, w_words, w_scales, twice_inv_d
         banks = [ps.tile([P, F], F32, name="bank%d" % b) for b in range(BANKS)]
         parked = out[0 : N // 2, :].bitcast(BF16).rearrange("r (two w) -> (r two) w", two=2)
 
-        early_scales = [sb.tile([P, 2, HALF], U8, name="early_scales%d" % h, align_bytes=64) for h in range(2)]
+        early_scales = [sb.tile([P, HALF], U8, name="early_scales%d" % g, align_bytes=64) for g in range(PASSES)]
         late_scales = sb.tile([P, PASSES, HALF], U8, align_bytes=64)
         early_w = [sb.tile([P, 2 * HALF], U8, name="early_w%d" % g, align_bytes=64) for g in range(PASSES)]
         late_w = [sb.tile([P, PASSES, HALF], U8, name="late_w%d" % h, align_bytes=64) for h in range(2)]
@@ -54,7 +56,7 @@ def tile_chebyshev_graph_filter_s13_kernel(tc, x, w_words, w_scales, twice_inv_d
         x_grouped = [sb.tile([P, F, PACK], BF16, name="x_grouped%d" % g, align_bytes=64) for g in range(PASSES)]
         x_codes = [sb.tile([P, F], U32, name="x_codes%d" % g, align_bytes=64) for g in range(PASSES)]
         x_scales = [sb.tile([P, F], U8, name="x_scales%d" % g, align_bytes=64) for g in range(PASSES)]
-        h_rows = [sb.tile([P, F], BF16, name="h_rows%d" % t) for t in range(TILES)]
+        h_rows = [sb.tile([P, F], BF16, name="h_rows%d" % t) for t in range(SORTED)]
         h_raw = [sb.tile([P, PACK * F], BF16, name="h_raw%d" % g) for g in range(PASSES)]
         h_grouped = [sb.tile([P, F, PACK], BF16, name="h_grouped%d" % g, align_bytes=64) for g in range(PASSES)]
         h_codes = [sb.tile([P, F], U32, name="h_codes%d" % g, align_bytes=64) for g in range(PASSES)]
@@ -65,6 +67,10 @@ def tile_chebyshev_graph_filter_s13_kernel(tc, x, w_words, w_scales, twice_inv_d
         zeros = sb.tile([P, P, PACK], BF16, align_bytes=64)
         zero_codes = sb.tile([P, P], U32, align_bytes=64)
         zero_scales = sb.tile([P, P], U8, align_bytes=64)
+        sorted_w = [sb.tile([P, PASSES, 2 * P], U8, name="sorted_w%d" % j, align_bytes=64) for j in range(PACK)]
+        sorted_scales = [sb.tile([P, PASSES, P], U8, name="sorted_scales%d" % j, align_bytes=64) for j in range(PACK)]
+        sorted_gain_rows = sb.tile([P, PACK], BF16)
+        sorted_gain = sb.tile([P, PACK], F32)
         gain = sb.tile([P, TILES], F32)
         minus_deg = sb.tile([P, TILES], F32)
 
@@ -72,15 +78,18 @@ def tile_chebyshev_graph_filter_s13_kernel(tc, x, w_words, w_scales, twice_inv_d
             if t < BANKS:
                 codes = early_w[g][:, 2 * P * t : 2 * P * (t + 1)]
                 cols = slice(P * t, P * (t + 1))
-                scales = early_scales[g // 2][:, g % 2, cols]
+                scales = early_scales[g][:, cols]
             else:
                 u = t - BANKS
                 codes = late_w[u // 4][:, g, 2 * P * (u % 4) : 2 * P * (u % 4 + 1)]
                 scales = late_scales[:, g, P * u : P * (u + 1)]
             return codes.bitcast(FP4X4), scales
 
-        def mx_pass(t, g, codes, scales):
-            w_codes, w_plane = w_operand(g, t)
+        def sorted_operand(g, t):
+            return sorted_w[t - SORTED][:, g, :].bitcast(FP4X4), sorted_scales[t - SORTED][:, g, :]
+
+        def mx_pass(t, g, codes, scales, operand=w_operand):
+            w_codes, w_plane = operand(g, t)
             nc.tensor.matmul_mx(
                 out=banks[t % BANKS][:],
                 lhsT=w_codes,
@@ -104,10 +113,11 @@ def tile_chebyshev_graph_filter_s13_kernel(tc, x, w_words, w_scales, twice_inv_d
                 nc.sync.dma_start(out=plane[r:P:32].bitcast(I32), in_=rows[r][:, passes, cols].bitcast(I32))
 
         nc.vector.memset(zeros[:], 0.0)
-        nc.vector.memset(early_scales[0][:].rearrange("p g n -> p (g n)").bitcast(I32), 0)
+        nc.vector.memset(early_scales[0][:].bitcast(I32), 0)
         quantise(zeros, zero_codes, zero_scales, 0, P)
-        for plane in [early_scales[1], late_scales]:
-            nc.vector.memset(plane[:].rearrange("p g n -> p (g n)").bitcast(I32), 0)
+        for g in range(1, PASSES):
+            nc.vector.memset(early_scales[g][:].bitcast(I32), 0)
+        nc.vector.memset(late_scales[:].rearrange("p g n -> p (g n)").bitcast(I32), 0)
         nc.gpsimd.memset(factor_rows[32:64, :], 0.0)
         nc.gpsimd.memset(factor_rows[64:P, :], 0.0)
         make_identity(nc, identity[:])
@@ -120,8 +130,7 @@ def tile_chebyshev_graph_filter_s13_kernel(tc, x, w_words, w_scales, twice_inv_d
             nc.sync.dma_start(out=x_raw[g][:], in_=x_by_word[g])
             rest = slice(2 * P if g == 0 else 0, 2 * HALF)
             nc.sync.dma_start(out=early_w[g][:, rest].bitcast(I32), in_=w_words[g][:, rest].bitcast(I32))
-            if g % 2 == 0:
-                load_scales(early_scales[g // 2], slice(g, g + 2), slice(0, HALF))
+            load_scales(early_scales[g], g, slice(0, HALF))
         load_scales(late_scales, slice(0, PASSES), slice(HALF, N))
         w_by_partition = w_words.rearrange("g p b -> p g b")
         for h in range(2):
@@ -129,6 +138,9 @@ def tile_chebyshev_graph_filter_s13_kernel(tc, x, w_words, w_scales, twice_inv_d
                 out=late_w[h][:].bitcast(I32),
                 in_=w_by_partition[:, :, (2 + h) * HALF : (3 + h) * HALF].bitcast(I32),
             )
+        nc.sync.dma_start(
+            out=sorted_gain_rows[:], in_=twice_inv_deg[P * SORTED : N].rearrange("(p t) -> p t", t=PACK)
+        )
 
         for r in range(WARM_UP):
             nc.tensor.matmul_mx(
@@ -165,7 +177,7 @@ def tile_chebyshev_graph_filter_s13_kernel(tc, x, w_words, w_scales, twice_inv_d
                 )
             else:
                 nc.scalar.activation(out=h_rows[t][:], in_=banks[t % BANKS][:], func=COPY, scale=gain[:, t : t + 1])
-            if t < TILES - 2:
+            if t not in DIRECT:
                 nc.sync.dma_start(out=parked[P * t : P * (t + 1), :], in_=h_rows[t][:])
             else:
                 q = t % PACK
@@ -189,24 +201,40 @@ def tile_chebyshev_graph_filter_s13_kernel(tc, x, w_words, w_scales, twice_inv_d
                 mx_pass(t, g, x_codes, x_scales)
         for t in range(BANKS):
             scale_and_park(t, t % 2 == 1)
-        for t in range(BANKS, TILES):
+        for j in range(PACK):
+            nc.vector.tensor_copy(
+                out=sorted_w[j][:].rearrange("p g (m b) -> p g m b", b=2),
+                in_=late_w[1][:].rearrange("p g (m t b) -> p g m t b", t=PACK, b=2)[:, :, :, j, :],
+            )
+            nc.vector.tensor_copy(
+                out=sorted_scales[j][:],
+                in_=late_scales[:, :, K_PASS:HALF].rearrange("p g (m t) -> p g m t", t=PACK)[:, :, :, j],
+            )
+        nc.vector.tensor_copy(out=sorted_gain[:], in_=sorted_gain_rows[:])
+        for t in range(BANKS, SORTED):
             for g in range(PASSES):
                 mx_pass(t, g, x_codes, x_scales)
-            if t == 8:
-                fetch(0, 0, P)
-                quantise_h(0, F)
-            if t == 9:
-                fetch(1, 0, P)
-                quantise_h(1, F)
-            if t == 14:
-                fetch(2, 0, P)
-                quantise_h(2, F)
-            if t == 15:
-                fetch(3, 0, 64)
+            if t < BANKS + 2:
+                fetch(t - BANKS, 0, P)
+                quantise_h(t - BANKS, F)
             scale_and_park(t, False)
+            if t >= BANKS + 2:
+                fetch(2, 32 * (t - BANKS - 2), 32 * (t - BANKS - 1))
+        fetch(2, 64, 96)
+        quantise_h(2, F)
         x_by_tile = x.rearrange("(g t p) f -> g p t f", p=P, t=PACK)
         for g in range(PASSES):
             nc.sync.dma_start(out=x_rows[g][:], in_=x_by_tile[g])
+        for t in range(SORTED, TILES):
+            j = t - SORTED
+            for g in range(PASSES):
+                mx_pass(t, g, x_codes, x_scales, sorted_operand)
+            nc.scalar.activation(
+                out=h_raw[PASSES - 1][:, F * j : F * (j + 1)],
+                in_=banks[t % BANKS][:],
+                func=COPY,
+                scale=sorted_gain[:, j : j + 1],
+            )
         quantise_h(3, SHARE)
 
         def finish(t, lo, hi):

@@ -18,22 +18,25 @@ ADD = mybir.AluOpType.add
 COPY = mybir.ActivationFunctionType.Copy
 
 P = 128
-PACK = 4
-K_PASS = P * PACK
-PASSES = N // K_PASS
+SLOTS = 4
+GROUP = P * SLOTS
+GROUPS = N // GROUP
 TILES = N // P
+QUARTER = P // SLOTS
+W_BYTES = 2
 BANKS = 8
-HALF = BANKS * P
+EARLY = BANKS * P
+SORTED = TILES - SLOTS
+DIRECT = SORTED - 1
 SHARE = 304
 WARM_UP = 14
-DIRECT = (11,)
-SORTED = TILES - PACK
+LAG = 4
 
 
 def interleave(copy, grouped, raw, lo, hi):
     copy(
         out=grouped[:, lo:hi, :].rearrange("p (c i) t -> p c t i", i=4),
-        in_=raw.rearrange("p t (c i) -> p c t i", i=4),
+        in_=raw[:, :, lo:hi].rearrange("p t (c i) -> p c t i", i=4),
     )
 
 
@@ -47,41 +50,40 @@ def tile_chebyshev_graph_filter_s13_kernel(tc, x, w_words, w_scales, twice_inv_d
         banks = [ps.tile([P, F], F32, name="bank%d" % b) for b in range(BANKS)]
         parked = out[0 : N // 2, :].bitcast(BF16).rearrange("r (two w) -> (r two) w", two=2)
 
-        early_scales = [sb.tile([P, HALF], U8, name="early_scales%d" % g, align_bytes=64) for g in range(PASSES)]
-        late_scales = sb.tile([P, PASSES, HALF], U8, align_bytes=64)
-        early_w = [sb.tile([P, 2 * HALF], U8, name="early_w%d" % g, align_bytes=64) for g in range(PASSES)]
-        late_w = [sb.tile([P, PASSES, HALF], U8, name="late_w%d" % h, align_bytes=64) for h in range(2)]
-        x_raw = [sb.tile([P, PACK, F], BF16, name="x_raw%d" % g) for g in range(PASSES)]
-        x_rows = [sb.tile([P, PACK, F], BF16, name="x_rows%d" % g) for g in range(PASSES)]
-        x_grouped = [sb.tile([P, F, PACK], BF16, name="x_grouped%d" % g, align_bytes=64) for g in range(PASSES)]
-        x_codes = [sb.tile([P, F], U32, name="x_codes%d" % g, align_bytes=64) for g in range(PASSES)]
-        x_scales = [sb.tile([P, F], U8, name="x_scales%d" % g, align_bytes=64) for g in range(PASSES)]
+        early_scales = [sb.tile([P, EARLY], U8, name="early_scales%d" % g, align_bytes=64) for g in range(GROUPS)]
+        late_scales = sb.tile([P, GROUPS, EARLY], U8, align_bytes=64)
+        early_w = [sb.tile([P, W_BYTES * EARLY], U8, name="early_w%d" % g, align_bytes=64) for g in range(GROUPS)]
+        late_w = [sb.tile([P, GROUPS, W_BYTES * GROUP], U8, name="late_w%d" % h, align_bytes=64) for h in range(2)]
+        x_raw = [sb.tile([P, SLOTS, F], BF16, name="x_raw%d" % g) for g in range(GROUPS)]
+        x_rows = [sb.tile([P, SLOTS, F], BF16, name="x_rows%d" % g) for g in range(GROUPS)]
+        x_grouped = [sb.tile([P, F, SLOTS], BF16, name="x_grouped%d" % g, align_bytes=64) for g in range(GROUPS)]
+        x_codes = [sb.tile([P, F], U32, name="x_codes%d" % g, align_bytes=64) for g in range(GROUPS)]
+        x_scales = [sb.tile([P, F], U8, name="x_scales%d" % g, align_bytes=64) for g in range(GROUPS)]
         h_rows = [sb.tile([P, F], BF16, name="h_rows%d" % t) for t in range(SORTED)]
-        h_raw = [sb.tile([P, PACK * F], BF16, name="h_raw%d" % g) for g in range(PASSES)]
-        h_grouped = [sb.tile([P, F, PACK], BF16, name="h_grouped%d" % g, align_bytes=64) for g in range(PASSES)]
-        h_codes = [sb.tile([P, F], U32, name="h_codes%d" % g, align_bytes=64) for g in range(PASSES)]
-        h_scales = [sb.tile([P, F], U8, name="h_scales%d" % g, align_bytes=64) for g in range(PASSES)]
+        h_raw = [sb.tile([P, SLOTS * F], BF16, name="h_raw%d" % g) for g in range(GROUPS)]
+        h_grouped = [sb.tile([P, F, SLOTS], BF16, name="h_grouped%d" % g, align_bytes=64) for g in range(GROUPS)]
+        h_codes = [sb.tile([P, F], U32, name="h_codes%d" % g, align_bytes=64) for g in range(GROUPS)]
+        h_scales = [sb.tile([P, F], U8, name="h_scales%d" % g, align_bytes=64) for g in range(GROUPS)]
         y_rows = [sb.tile([P, F], F32, name="y_rows%d" % t) for t in range(TILES)]
         factor_rows = sb.tile([P, P], BF16)
         identity = sb.tile([P, P], BF16)
-        zeros = sb.tile([P, P, PACK], BF16, align_bytes=64)
+        zeros = sb.tile([P, P, SLOTS], BF16, align_bytes=64)
         zero_codes = sb.tile([P, P], U32, align_bytes=64)
         zero_scales = sb.tile([P, P], U8, align_bytes=64)
-        sorted_w = [sb.tile([P, PASSES, 2 * P], U8, name="sorted_w%d" % j, align_bytes=64) for j in range(PACK)]
-        sorted_scales = [sb.tile([P, PASSES, P], U8, name="sorted_scales%d" % j, align_bytes=64) for j in range(PACK)]
-        sorted_gain_rows = sb.tile([P, PACK], BF16)
-        sorted_gain = sb.tile([P, PACK], F32)
+        sorted_w = [sb.tile([P, GROUPS, W_BYTES * P], U8, name="sorted_w%d" % j, align_bytes=64) for j in range(SLOTS)]
+        sorted_scales = [sb.tile([P, GROUPS, P], U8, name="sorted_scales%d" % j, align_bytes=64) for j in range(SLOTS)]
+        sorted_gain_bf16 = sb.tile([P, SLOTS], BF16)
+        sorted_gain = sb.tile([P, SLOTS], F32)
         gain = sb.tile([P, TILES], F32)
         minus_deg = sb.tile([P, TILES], F32)
 
         def w_operand(g, t):
             if t < BANKS:
-                codes = early_w[g][:, 2 * P * t : 2 * P * (t + 1)]
-                cols = slice(P * t, P * (t + 1))
-                scales = early_scales[g][:, cols]
+                codes = early_w[g][:, W_BYTES * P * t : W_BYTES * P * (t + 1)]
+                scales = early_scales[g][:, P * t : P * (t + 1)]
             else:
                 u = t - BANKS
-                codes = late_w[u // 4][:, g, 2 * P * (u % 4) : 2 * P * (u % 4 + 1)]
+                codes = late_w[u // SLOTS][:, g, W_BYTES * P * (u % SLOTS) : W_BYTES * P * (u % SLOTS + 1)]
                 scales = late_scales[:, g, P * u : P * (u + 1)]
             return codes.bitcast(FP4X4), scales
 
@@ -97,7 +99,7 @@ def tile_chebyshev_graph_filter_s13_kernel(tc, x, w_words, w_scales, twice_inv_d
                 rhs=codes[g][:].bitcast(FP8X4),
                 rhs_scale=scales[g][:],
                 start=(g == 0),
-                stop=(g == PASSES - 1),
+                stop=(g == GROUPS - 1),
             )
 
         def quantise(grouped, codes, scales, lo, hi):
@@ -107,45 +109,56 @@ def tile_chebyshev_graph_filter_s13_kernel(tc, x, w_words, w_scales, twice_inv_d
                 in_=grouped[:, lo:hi, :].rearrange("p f t -> p (f t)"),
             )
 
-        def load_scales(plane, passes, cols):
+        def pack_operand(raw, grouped, codes, scales, share):
+            half = F // 2
+            interleave(nc.vector.tensor_copy, grouped, raw, 0, half)
+            interleave(nc.vector.tensor_copy, grouped, raw, half, share)
+            if share < F:
+                interleave(nc.scalar.copy, grouped, raw, share, F)
+            quantise(grouped, codes, scales, 0, half)
+            quantise(grouped, codes, scales, half, F)
+
+        def load_scales(plane, groups, cols):
             rows = w_scales.rearrange("g (q r) n -> r q g n", r=4)
             for r in range(4):
-                nc.sync.dma_start(out=plane[r:P:32].bitcast(I32), in_=rows[r][:, passes, cols].bitcast(I32))
+                nc.sync.dma_start(out=plane[r:P:32].bitcast(I32), in_=rows[r][:, groups, cols].bitcast(I32))
 
         nc.vector.memset(zeros[:], 0.0)
         nc.vector.memset(early_scales[0][:].bitcast(I32), 0)
         quantise(zeros, zero_codes, zero_scales, 0, P)
-        for g in range(1, PASSES):
+        for g in range(1, GROUPS):
             nc.vector.memset(early_scales[g][:].bitcast(I32), 0)
         nc.vector.memset(late_scales[:].rearrange("p g n -> p (g n)").bitcast(I32), 0)
+
         nc.gpsimd.memset(factor_rows[32:64, :], 0.0)
         nc.gpsimd.memset(factor_rows[64:P, :], 0.0)
         make_identity(nc, identity[:])
         nc.scalar.dma_start(out=factor_rows[0:TILES, :], in_=twice_inv_deg.rearrange("(t p) -> t p", p=P))
         nc.scalar.dma_start(out=factor_rows[TILES : 2 * TILES, :], in_=deg.rearrange("(t p) -> t p", p=P))
 
-        x_by_word = x.rearrange("(g p t) f -> g p t f", p=P, t=PACK)
-        nc.sync.dma_start(out=early_w[0][:, 0 : 2 * P].bitcast(I32), in_=w_words[0][:, 0 : 2 * P].bitcast(I32))
-        for g in range(PASSES):
+        x_by_word = x.rearrange("(g p t) f -> g p t f", p=P, t=SLOTS)
+        first = slice(0, W_BYTES * P)
+        nc.sync.dma_start(out=early_w[0][:, first].bitcast(I32), in_=w_words[0][:, first].bitcast(I32))
+        for g in range(GROUPS):
             nc.sync.dma_start(out=x_raw[g][:], in_=x_by_word[g])
-            rest = slice(2 * P if g == 0 else 0, 2 * HALF)
+            rest = slice(first.stop if g == 0 else 0, W_BYTES * EARLY)
             nc.sync.dma_start(out=early_w[g][:, rest].bitcast(I32), in_=w_words[g][:, rest].bitcast(I32))
-            load_scales(early_scales[g], g, slice(0, HALF))
-        load_scales(late_scales, slice(0, PASSES), slice(HALF, N))
+            load_scales(early_scales[g], g, slice(0, EARLY))
+        load_scales(late_scales, slice(0, GROUPS), slice(EARLY, N))
         w_by_partition = w_words.rearrange("g p b -> p g b")
         for h in range(2):
+            lo = W_BYTES * (EARLY + h * GROUP)
             nc.sync.dma_start(
-                out=late_w[h][:].bitcast(I32),
-                in_=w_by_partition[:, :, (2 + h) * HALF : (3 + h) * HALF].bitcast(I32),
+                out=late_w[h][:].bitcast(I32), in_=w_by_partition[:, :, lo : lo + W_BYTES * GROUP].bitcast(I32)
             )
         nc.sync.dma_start(
-            out=sorted_gain_rows[:], in_=twice_inv_deg[P * SORTED : N].rearrange("(p t) -> p t", t=PACK)
+            out=sorted_gain_bf16[:], in_=twice_inv_deg[P * SORTED : N].rearrange("(p t) -> p t", t=SLOTS)
         )
 
-        for r in range(WARM_UP):
+        for repeat in range(WARM_UP):
             nc.tensor.matmul_mx(
                 out=banks[0][:, 0:P],
-                lhsT=early_w[0][:, 0 : 2 * P].bitcast(FP4X4),
+                lhsT=early_w[0][:, first].bitcast(FP4X4),
                 lhsT_scale=zero_scales[:],
                 rhs=zero_codes[:].bitcast(FP8X4),
                 rhs_scale=zero_scales[:],
@@ -155,92 +168,88 @@ def tile_chebyshev_graph_filter_s13_kernel(tc, x, w_words, w_scales, twice_inv_d
         turned = banks[BANKS - 1][:].bitcast(BF16)[:, 0:P]
         nc.tensor.transpose(turned, factor_rows[:], identity[:])
 
-        def pack_operand(raw, grouped, codes, scales, split):
-            half = F // 2
-            interleave(nc.vector.tensor_copy, grouped, raw[:, :, 0:half], 0, half)
-            interleave(nc.vector.tensor_copy, grouped, raw[:, :, half:split], half, split)
-            if split < F:
-                interleave(nc.scalar.copy, grouped, raw[:, :, split:F], split, F)
-            quantise(grouped, codes, scales, 0, half)
-            quantise(grouped, codes, scales, half, F)
-
-        for g in range(PASSES):
+        for g in range(GROUPS):
             pack_operand(x_raw[g][:], x_grouped[g], x_codes[g], x_scales[g], SHARE)
             if g == 0:
                 nc.scalar.activation(out=gain[:], in_=turned[:, 0:TILES], func=COPY)
                 nc.scalar.activation(out=minus_deg[:], in_=turned[:, TILES : 2 * TILES], func=COPY, scale=-1.0)
 
-        def scale_and_park(t, on_vector):
+        def scale_and_move(t, on_vector):
             if on_vector:
                 nc.vector.tensor_scalar(
                     out=h_rows[t][:], in0=banks[t % BANKS][:], scalar1=gain[:, t : t + 1], scalar2=None, op0=MULT
                 )
             else:
                 nc.scalar.activation(out=h_rows[t][:], in_=banks[t % BANKS][:], func=COPY, scale=gain[:, t : t + 1])
-            if t not in DIRECT:
+            if t != DIRECT:
                 nc.sync.dma_start(out=parked[P * t : P * (t + 1), :], in_=h_rows[t][:])
             else:
-                q = t % PACK
-                for j in range(PACK):
+                lo = QUARTER * (t % SLOTS)
+                for j in range(SLOTS):
                     nc.sync.dma_start(
-                        out=h_raw[t // PACK][32 * q : 32 * (q + 1), F * j : F * (j + 1)], in_=h_rows[t][j:P:PACK, :]
+                        out=h_raw[t // SLOTS][lo : lo + QUARTER, F * j : F * (j + 1)], in_=h_rows[t][j:P:SLOTS, :]
                     )
 
-        def fetch(g, lo, hi):
-            rows = parked[K_PASS * g + PACK * lo : K_PASS * g + PACK * hi, :]
+        def fetch(t, count):
+            lo = QUARTER * (t % SLOTS)
             nc.sync.dma_start(
-                out=h_raw[g][lo:hi, :], in_=rows.rearrange("(p t) w -> p (t w)", t=PACK)
+                out=h_raw[t // SLOTS][lo : lo + QUARTER * count, :],
+                in_=parked[P * t : P * (t + count), :].rearrange("(p t) w -> p (t w)", t=SLOTS),
             )
 
-        def quantise_h(g, split):
-            raw = h_raw[g][:].rearrange("p (t f) -> p t f", t=PACK)
-            pack_operand(raw, h_grouped[g], h_codes[g], h_scales[g], split)
+        def quantise_h(g, share):
+            raw = h_raw[g][:].rearrange("p (t f) -> p t f", t=SLOTS)
+            pack_operand(raw, h_grouped[g], h_codes[g], h_scales[g], share)
 
-        for g in range(PASSES):
+        for g in range(GROUPS):
             for t in range(BANKS):
                 mx_pass(t, g, x_codes, x_scales)
         for t in range(BANKS):
-            scale_and_park(t, t % 2 == 1)
-        for j in range(PACK):
+            scale_and_move(t, t % 2 == 1)
+
+        for j in range(SLOTS):
             nc.vector.tensor_copy(
-                out=sorted_w[j][:].rearrange("p g (m b) -> p g m b", b=2),
-                in_=late_w[1][:].rearrange("p g (m t b) -> p g m t b", t=PACK, b=2)[:, :, :, j, :],
+                out=sorted_w[j][:].rearrange("p g (m b) -> p g m b", b=W_BYTES),
+                in_=late_w[1][:].rearrange("p g (m t b) -> p g m t b", t=SLOTS, b=W_BYTES)[:, :, :, j, :],
             )
             nc.vector.tensor_copy(
                 out=sorted_scales[j][:],
-                in_=late_scales[:, :, K_PASS:HALF].rearrange("p g (m t) -> p g m t", t=PACK)[:, :, :, j],
+                in_=late_scales[:, :, GROUP:EARLY].rearrange("p g (m t) -> p g m t", t=SLOTS)[:, :, :, j],
             )
-        nc.vector.tensor_copy(out=sorted_gain[:], in_=sorted_gain_rows[:])
+        nc.vector.tensor_copy(out=sorted_gain[:], in_=sorted_gain_bf16[:])
+
         for t in range(BANKS, SORTED):
-            for g in range(PASSES):
+            for g in range(GROUPS):
                 mx_pass(t, g, x_codes, x_scales)
             if t < BANKS + 2:
-                fetch(t - BANKS, 0, P)
+                fetch(SLOTS * (t - BANKS), SLOTS)
                 quantise_h(t - BANKS, F)
-            scale_and_park(t, False)
+            scale_and_move(t, False)
             if t >= BANKS + 2:
-                fetch(2, 32 * (t - BANKS - 2), 32 * (t - BANKS - 1))
-        fetch(2, 64, 96)
-        quantise_h(2, F)
-        x_by_tile = x.rearrange("(g t p) f -> g p t f", p=P, t=PACK)
-        for g in range(PASSES):
+                fetch(t - 2, 1)
+        fetch(DIRECT - 1, 1)
+
+        x_by_tile = x.rearrange("(g t p) f -> g p t f", p=P, t=SLOTS)
+        for g in range(GROUPS):
             nc.sync.dma_start(out=x_rows[g][:], in_=x_by_tile[g])
+
         for t in range(SORTED, TILES):
             j = t - SORTED
-            for g in range(PASSES):
+            for g in range(GROUPS):
                 mx_pass(t, g, x_codes, x_scales, sorted_operand)
             nc.scalar.activation(
-                out=h_raw[PASSES - 1][:, F * j : F * (j + 1)],
+                out=h_raw[GROUPS - 1][:, F * j : F * (j + 1)],
                 in_=banks[t % BANKS][:],
                 func=COPY,
                 scale=sorted_gain[:, j : j + 1],
             )
-        quantise_h(3, SHARE)
+        for g in range(2, GROUPS):
+            quantise_h(g, SHARE)
 
         def finish(t, lo, hi):
             nc.vector.scalar_tensor_tensor(
                 out=y_rows[t][:, lo:hi],
-                in0=x_rows[t // PACK][:, t % PACK, lo:hi],
+                in0=x_rows[t // SLOTS][:, t % SLOTS, lo:hi],
                 scalar=minus_deg[:, t : t + 1],
                 in1=banks[t % BANKS][:, lo:hi],
                 op0=MULT,
@@ -248,13 +257,17 @@ def tile_chebyshev_graph_filter_s13_kernel(tc, x, w_words, w_scales, twice_inv_d
             )
             nc.sync.dma_start(out=out[P * t : P * (t + 1), lo:hi], in_=y_rows[t][:, lo:hi])
 
-        for g in range(PASSES):
+        for g in range(GROUPS - 2):
             for t in range(BANKS):
                 mx_pass(t, g, h_codes, h_scales)
-        for t in range(BANKS):
-            finish(t, 0, F)
+        for step in range(BANKS + LAG):
+            if step < BANKS:
+                mx_pass(step, GROUPS - 2, h_codes, h_scales)
+            if step >= LAG:
+                mx_pass(step - LAG, GROUPS - 1, h_codes, h_scales)
+                finish(step - LAG, 0, F)
         for t in range(BANKS, TILES):
-            for g in range(PASSES):
+            for g in range(GROUPS):
                 mx_pass(t, g, h_codes, h_scales)
             if t < TILES - 1:
                 finish(t, 0, F)

from contextlib import ExitStack

import concourse.mybir as mybir
from concourse.masks import make_identity

N, F = 2048, 512
FLOPS = 2 * 2 * N * N * F

F32 = mybir.dt.float32
BF16 = mybir.dt.bfloat16
I32 = mybir.dt.int32
U32 = mybir.dt.uint32
U8 = mybir.dt.uint8
FP8X4 = mybir.dt.float8_e4m3fn_x4
FP4X4 = mybir.dt.float4_e2m1fn_x4
MULT = mybir.AluOpType.mult
ADD = mybir.AluOpType.add
COPY = mybir.ActivationFunctionType.Copy

P = 128
SLOTS = 4
GROUP = P * SLOTS
GROUPS = N // GROUP
TILES = N // P
QUARTER = P // SLOTS
W_BYTES = 2
BANKS = 8
EARLY = BANKS * P
SORTED = TILES - SLOTS
DIRECT = SORTED - 1
SHARE = 304
WARM_UP = 14
LAG = 4


def interleave(copy, grouped, raw, lo, hi):
    copy(
        out=grouped[:, lo:hi, :].rearrange("p (c i) t -> p c t i", i=4),
        in_=raw[:, :, lo:hi].rearrange("p t (c i) -> p c t i", i=4),
    )


def tile_chebyshev_graph_filter_s13_kernel(tc, x, w_words, w_scales, twice_inv_deg, deg, out):
    nc = tc.nc
    with ExitStack() as ctx:
        sb = ctx.enter_context(tc.tile_pool(name="sb", bufs=1))
        ps = ctx.enter_context(tc.psum_pool(name="ps", bufs=1))
        ctx.enter_context(tc.manual_schedule())

        banks = [ps.tile([P, F], F32, name="bank%d" % b) for b in range(BANKS)]
        parked = out[0 : N // 2, :].bitcast(BF16).rearrange("r (two w) -> (r two) w", two=2)

        early_scales = [sb.tile([P, EARLY], U8, name="early_scales%d" % g, align_bytes=64) for g in range(GROUPS)]
        late_scales = sb.tile([P, GROUPS, EARLY], U8, align_bytes=64)
        early_w = [sb.tile([P, W_BYTES * EARLY], U8, name="early_w%d" % g, align_bytes=64) for g in range(GROUPS)]
        late_w = [sb.tile([P, GROUPS, W_BYTES * GROUP], U8, name="late_w%d" % h, align_bytes=64) for h in range(2)]
        x_raw = [sb.tile([P, SLOTS, F], BF16, name="x_raw%d" % g) for g in range(GROUPS)]
        x_rows = [sb.tile([P, SLOTS, F], BF16, name="x_rows%d" % g) for g in range(GROUPS)]
        x_grouped = [sb.tile([P, F, SLOTS], BF16, name="x_grouped%d" % g, align_bytes=64) for g in range(GROUPS)]
        x_codes = [sb.tile([P, F], U32, name="x_codes%d" % g, align_bytes=64) for g in range(GROUPS)]
        x_scales = [sb.tile([P, F], U8, name="x_scales%d" % g, align_bytes=64) for g in range(GROUPS)]
        h_rows = [sb.tile([P, F], BF16, name="h_rows%d" % t) for t in range(SORTED)]
        h_raw = [sb.tile([P, SLOTS * F], BF16, name="h_raw%d" % g) for g in range(GROUPS)]
        h_grouped = [sb.tile([P, F, SLOTS], BF16, name="h_grouped%d" % g, align_bytes=64) for g in range(GROUPS)]
        h_codes = [sb.tile([P, F], U32, name="h_codes%d" % g, align_bytes=64) for g in range(GROUPS)]
        h_scales = [sb.tile([P, F], U8, name="h_scales%d" % g, align_bytes=64) for g in range(GROUPS)]
        y_rows = [sb.tile([P, F], F32, name="y_rows%d" % t) for t in range(TILES)]
        factor_rows = sb.tile([P, P], BF16)
        identity = sb.tile([P, P], BF16)
        zeros = sb.tile([P, P, SLOTS], BF16, align_bytes=64)
        zero_codes = sb.tile([P, P], U32, align_bytes=64)
        zero_scales = sb.tile([P, P], U8, align_bytes=64)
        sorted_w = [sb.tile([P, GROUPS, W_BYTES * P], U8, name="sorted_w%d" % j, align_bytes=64) for j in range(SLOTS)]
        sorted_scales = [sb.tile([P, GROUPS, P], U8, name="sorted_scales%d" % j, align_bytes=64) for j in range(SLOTS)]
        sorted_gain_bf16 = sb.tile([P, SLOTS], BF16)
        sorted_gain = sb.tile([P, SLOTS], F32)
        gain = sb.tile([P, TILES], F32)
        minus_deg = sb.tile([P, TILES], F32)

        def w_operand(g, t):
            if t < BANKS:
                codes = early_w[g][:, W_BYTES * P * t : W_BYTES * P * (t + 1)]
                scales = early_scales[g][:, P * t : P * (t + 1)]
            else:
                u = t - BANKS
                codes = late_w[u // SLOTS][:, g, W_BYTES * P * (u % SLOTS) : W_BYTES * P * (u % SLOTS + 1)]
                scales = late_scales[:, g, P * u : P * (u + 1)]
            return codes.bitcast(FP4X4), scales

        def sorted_operand(g, t):
            return sorted_w[t - SORTED][:, g, :].bitcast(FP4X4), sorted_scales[t - SORTED][:, g, :]

        def mx_pass(t, g, codes, scales, operand=w_operand):
            w_codes, w_plane = operand(g, t)
            nc.tensor.matmul_mx(
                out=banks[t % BANKS][:],
                lhsT=w_codes,
                lhsT_scale=w_plane,
                rhs=codes[g][:].bitcast(FP8X4),
                rhs_scale=scales[g][:],
                start=(g == 0),
                stop=(g == GROUPS - 1),
            )

        def quantise(grouped, codes, scales, lo, hi):
            nc.vector.quantize_mx(
                out=codes[:, lo:hi].bitcast(FP8X4),
                scales=scales[:, lo:hi],
                in_=grouped[:, lo:hi, :].rearrange("p f t -> p (f t)"),
            )

        def pack_operand(raw, grouped, codes, scales, share):
            half = F // 2
            interleave(nc.vector.tensor_copy, grouped, raw, 0, half)
            interleave(nc.vector.tensor_copy, grouped, raw, half, share)
            if share < F:
                interleave(nc.scalar.copy, grouped, raw, share, F)
            quantise(grouped, codes, scales, 0, half)
            quantise(grouped, codes, scales, half, F)

        def load_scales(plane, groups, cols):
            rows = w_scales.rearrange("g (q r) n -> r q g n", r=4)
            for r in range(4):
                nc.sync.dma_start(out=plane[r:P:32].bitcast(I32), in_=rows[r][:, groups, cols].bitcast(I32))

        nc.vector.memset(zeros[:], 0.0)
        nc.vector.memset(early_scales[0][:].bitcast(I32), 0)
        quantise(zeros, zero_codes, zero_scales, 0, P)
        for g in range(1, GROUPS):
            nc.vector.memset(early_scales[g][:].bitcast(I32), 0)
        nc.vector.memset(late_scales[:].rearrange("p g n -> p (g n)").bitcast(I32), 0)

        nc.gpsimd.memset(factor_rows[32:64, :], 0.0)
        nc.gpsimd.memset(factor_rows[64:P, :], 0.0)
        make_identity(nc, identity[:])
        nc.scalar.dma_start(out=factor_rows[0:TILES, :], in_=twice_inv_deg.rearrange("(t p) -> t p", p=P))
        nc.scalar.dma_start(out=factor_rows[TILES : 2 * TILES, :], in_=deg.rearrange("(t p) -> t p", p=P))

        x_by_word = x.rearrange("(g p t) f -> g p t f", p=P, t=SLOTS)
        first = slice(0, W_BYTES * P)
        nc.sync.dma_start(out=early_w[0][:, first].bitcast(I32), in_=w_words[0][:, first].bitcast(I32))
        for g in range(GROUPS):
            nc.sync.dma_start(out=x_raw[g][:], in_=x_by_word[g])
            rest = slice(first.stop if g == 0 else 0, W_BYTES * EARLY)
            nc.sync.dma_start(out=early_w[g][:, rest].bitcast(I32), in_=w_words[g][:, rest].bitcast(I32))
            load_scales(early_scales[g], g, slice(0, EARLY))
        load_scales(late_scales, slice(0, GROUPS), slice(EARLY, N))
        w_by_partition = w_words.rearrange("g p b -> p g b")
        for h in range(2):
            lo = W_BYTES * (EARLY + h * GROUP)
            nc.sync.dma_start(
                out=late_w[h][:].bitcast(I32), in_=w_by_partition[:, :, lo : lo + W_BYTES * GROUP].bitcast(I32)
            )
        nc.sync.dma_start(
            out=sorted_gain_bf16[:], in_=twice_inv_deg[P * SORTED : N].rearrange("(p t) -> p t", t=SLOTS)
        )

        for repeat in range(WARM_UP):
            nc.tensor.matmul_mx(
                out=banks[0][:, 0:P],
                lhsT=early_w[0][:, first].bitcast(FP4X4),
                lhsT_scale=zero_scales[:],
                rhs=zero_codes[:].bitcast(FP8X4),
                rhs_scale=zero_scales[:],
                start=True,
                stop=True,
            )
        turned = banks[BANKS - 1][:].bitcast(BF16)[:, 0:P]
        nc.tensor.transpose(turned, factor_rows[:], identity[:])

        for g in range(GROUPS):
            pack_operand(x_raw[g][:], x_grouped[g], x_codes[g], x_scales[g], SHARE)
            if g == 0:
                nc.scalar.activation(out=gain[:], in_=turned[:, 0:TILES], func=COPY)
                nc.scalar.activation(out=minus_deg[:], in_=turned[:, TILES : 2 * TILES], func=COPY, scale=-1.0)

        def scale_and_move(t, on_vector):
            if on_vector:
                nc.vector.tensor_scalar(
                    out=h_rows[t][:], in0=banks[t % BANKS][:], scalar1=gain[:, t : t + 1], scalar2=None, op0=MULT
                )
            else:
                nc.scalar.activation(out=h_rows[t][:], in_=banks[t % BANKS][:], func=COPY, scale=gain[:, t : t + 1])
            if t != DIRECT:
                nc.sync.dma_start(out=parked[P * t : P * (t + 1), :], in_=h_rows[t][:])
            else:
                lo = QUARTER * (t % SLOTS)
                for j in range(SLOTS):
                    nc.sync.dma_start(
                        out=h_raw[t // SLOTS][lo : lo + QUARTER, F * j : F * (j + 1)], in_=h_rows[t][j:P:SLOTS, :]
                    )

        def fetch(t, count):
            lo = QUARTER * (t % SLOTS)
            nc.sync.dma_start(
                out=h_raw[t // SLOTS][lo : lo + QUARTER * count, :],
                in_=parked[P * t : P * (t + count), :].rearrange("(p t) w -> p (t w)", t=SLOTS),
            )

        def quantise_h(g, share):
            raw = h_raw[g][:].rearrange("p (t f) -> p t f", t=SLOTS)
            pack_operand(raw, h_grouped[g], h_codes[g], h_scales[g], share)

        for g in range(GROUPS):
            for t in range(BANKS):
                mx_pass(t, g, x_codes, x_scales)
        for t in range(BANKS):
            scale_and_move(t, t % 2 == 1)

        for j in range(SLOTS):
            nc.vector.tensor_copy(
                out=sorted_w[j][:].rearrange("p g (m b) -> p g m b", b=W_BYTES),
                in_=late_w[1][:].rearrange("p g (m t b) -> p g m t b", t=SLOTS, b=W_BYTES)[:, :, :, j, :],
            )
            nc.vector.tensor_copy(
                out=sorted_scales[j][:],
                in_=late_scales[:, :, GROUP:EARLY].rearrange("p g (m t) -> p g m t", t=SLOTS)[:, :, :, j],
            )
        nc.vector.tensor_copy(out=sorted_gain[:], in_=sorted_gain_bf16[:])

        for t in range(BANKS, SORTED):
            for g in range(GROUPS):
                mx_pass(t, g, x_codes, x_scales)
            if t < BANKS + 2:
                fetch(SLOTS * (t - BANKS), SLOTS)
                quantise_h(t - BANKS, F)
            scale_and_move(t, False)
            if t >= BANKS + 2:
                fetch(t - 2, 1)
        fetch(DIRECT - 1, 1)

        x_by_tile = x.rearrange("(g t p) f -> g p t f", p=P, t=SLOTS)
        for g in range(GROUPS):
            nc.sync.dma_start(out=x_rows[g][:], in_=x_by_tile[g])

        for t in range(SORTED, TILES):
            j = t - SORTED
            for g in range(GROUPS):
                mx_pass(t, g, x_codes, x_scales, sorted_operand)
            nc.scalar.activation(
                out=h_raw[GROUPS - 1][:, F * j : F * (j + 1)],
                in_=banks[t % BANKS][:],
                func=COPY,
                scale=sorted_gain[:, j : j + 1],
            )
        for g in range(2, GROUPS):
            quantise_h(g, SHARE)

        def finish(t, lo, hi):
            nc.vector.scalar_tensor_tensor(
                out=y_rows[t][:, lo:hi],
                in0=x_rows[t // SLOTS][:, t % SLOTS, lo:hi],
                scalar=minus_deg[:, t : t + 1],
                in1=banks[t % BANKS][:, lo:hi],
                op0=MULT,
                op1=ADD,
            )
            nc.sync.dma_start(out=out[P * t : P * (t + 1), lo:hi], in_=y_rows[t][:, lo:hi])

        for g in range(GROUPS - 2):
            for t in range(BANKS):
                mx_pass(t, g, h_codes, h_scales)
        for step in range(BANKS + LAG):
            if step < BANKS:
                mx_pass(step, GROUPS - 2, h_codes, h_scales)
            if step >= LAG:
                mx_pass(step - LAG, GROUPS - 1, h_codes, h_scales)
                finish(step - LAG, 0, F)
        for t in range(BANKS, TILES):
            for g in range(GROUPS):
                mx_pass(t, g, h_codes, h_scales)
            if t < TILES - 1:
                finish(t, 0, F)
            else:
                finish(t, 0, F // 2)
                finish(t, F // 2, F)
